import numpy as np
CORES = [51,54,179,182]
N = 4
T, CAP, KR = 256, 96, 4096
def entries(a): return a.T.reshape(-1)
def pack(v, P): return np.ascontiguousarray(np.asarray(v, np.int32).reshape(-1, P).T)
def lists(rng, how):
    D = np.stack([rng.permutation(np.repeat(np.arange(N), CAP))[:T] for r in range(N)])
    if how == "full": D = np.stack([(lambda q: rng.permutation(np.concatenate([np.repeat(q[:T // CAP], CAP), np.repeat(q[T // CAP:T // CAP + 1], T % CAP)])))(rng.permutation(N)) for r in range(N)])
    if how == "sorted": D = np.sort(D, axis=1)
    if how == "none": z = int(rng.integers(N)); D = np.stack([rng.permutation(np.repeat(np.delete(np.arange(N), z), CAP))[:T] for r in range(N)]) if CAP * (N - 1) >= T else D
    K_ = KR * D + (np.where(rng.random((N, T)) < 0.5, 0, KR - 1) if how == "edge" else rng.integers(0, KR, (N, T)))
    return {"key": np.stack([pack(K_[r], 16) for r in range(N)])}
def setup_inputs(rng):
    return dict({"x": rng.standard_normal((N, 128, T), dtype=np.float32)}, **lists(rng, "uniform"))
def setup_inputs_edge(rng):
    d = setup_inputs(rng); d.update(lists(rng, "edge"))
    for k in ("x",): d[k] = (d[k].astype(np.float32) * 1048576.0).astype(d[k].dtype)
    return d
def setup_inputs_full(rng):
    d = setup_inputs(rng); d.update(lists(rng, "full"))
    for k in ("x",): d[k] = (d[k].astype(np.float32) * (1 / 1024.0)).astype(d[k].dtype)
    return d
def setup_inputs_none(rng):
    d = setup_inputs(rng); d.update(lists(rng, "none"))
    return d
def setup_inputs_sorted(rng):
    d = setup_inputs(rng); d.update(lists(rng, "sorted"))
    return d
def check_inputs(x):
    bad = []
    if x["key"].min() < 0 or x["key"].max() >= N * KR: bad.append("key out of range")
    if max(int(np.bincount(entries(a) // KR, minlength=N).max()) for a in x["key"]) > CAP: bad.append("more than CAP columns of a rank go to one rank")
    return bad
def reference(x, key):
    y = np.zeros((N, 128, N * CAP), x.dtype)
    for r in range(N):
        D = entries(key[r]) // KR
        for d in range(N):
            got = x[r][:, D == d]; y[d][:, CAP * r:CAP * r + got.shape[1]] = got
    return {"y": y}

@@ -1,0 +1,176 @@
+from concourse.bass import DstId, RemoteDMATransfer
+from concourse.mybir import AluOpType
+
+N, CAP, TCOL, KR = 4, 96, 256, 4096
+NEAR_SHARE = 8
+
+SCRATCH = {
+    "xs": ("sbuf", [128, TCOL], "float32"),
+    "send": ("sbuf", [128, N * CAP], "float32"),
+    "land": ("sbuf", [128, N * CAP], "float32"),
+    "key64": ("sbuf", [64, 16], "int32"),
+    "loi": ("sbuf", [64, 1], "int32"),
+    "lom": ("sbuf", [64, 1], "int32"),
+    "lo": ("sbuf", [64, 1], "float32"),
+    "init": ("sbuf", [64, 1], "float32"),
+    "z": ("sbuf", [64, 192], "int32"),
+    "zs": ("sbuf", [64, 192], "int32"),
+    "e": ("sbuf", [64, 192], "bfloat16"),
+    "l1": ("sbuf", [64, 64], "bfloat16"),
+    "l2": ("sbuf", [64, 64], "bfloat16"),
+    "zr": ("sbuf", [64, 128], "int32"),
+    "zra": ("sbuf", [64, 128], "int32"),
+    "rep": ("sbuf", [64, 128], "bfloat16"),
+    "gp": ("sbuf", [64, 17], "bfloat16"),
+    "g2": ("sbuf", [64, 16], "bfloat16"),
+    "oh": ("sbuf", [64, 16], "bfloat16"),
+    "zero16": ("sbuf", [64, 16], "float32"),
+    "q": ("sbuf", [64, 16], "bfloat16"),
+    "prod": ("sbuf", [64, 16], "bfloat16"),
+    "off": ("sbuf", [128, 16], "uint16"),
+    "pd": ("psum", [128, 512], "float32"),
+    "ps": ("psum", [128, 512], "float32"),
+}
+SEMAPHORES = ["keys", "xin", "i_lo", "i_z", "i_zr", "m_send", "m_small", "c_lom", "c_lo", "c_init", "c_zs", "c_e", "c_l",
+              "c_zra", "c_rep", "v_g", "v_g2", "v_oh", "t_d", "v_q", "v_prod", "t_s", "v_off", "v_scat", "v_own",
+              "left", "a_near", "a_far", "st_near", "st_far"]
+
+
+def _bits(mask):
+    return [e for e in range(mask.bit_length()) if (mask >> e) & 1]
+
+
+def _pow2(n):
+    p = 1
+    while p * 2 <= n:
+        p *= 2
+    return p
+
+
+def _same_chip(topo, a, b):
+    return topo.host(a) == topo.host(b) and topo.chip(a) == topo.chip(b)
+
+
+def _plan(topo, cores, src):
+    far = [c for c in cores if c != src and not _same_chip(topo, src, c)]
+    near = [c for c in cores if c != src and _same_chip(topo, src, c)]
+    used, plan = [], {}
+    for group, cap in ((far, None), (near, NEAR_SHARE)):
+        left = len(group)
+        for dst in group:
+            free = [e for e in _bits(topo.mask(src, dst)) if e not in used]
+            n = _pow2(len(free) // left)
+            if cap is not None:
+                n = min(n, cap)
+            plan[dst] = free[:n]
+            used += free[:n]
+            left -= 1
+    return plan
+
+
+def _runs(ranks):
+    out = []
+    for r in sorted(ranks):
+        if out and out[-1][1] == r:
+            out[-1][1] = r + 1
+        else:
+            out.append([r, r + 1])
+    return out
+
+
+def rank_program(g, core, T, topo):
+    rank = T.rank_of(core)
+    if rank is None:
+        return
+    S, V, PE, A = T.sem, g.vector, g.tensor, AluOpType
+    cores = list(T.cores)
+
+    g.sync.dma_start(T.key64[0:16, :], T.key[:, :]).then_inc(S.keys, 16)
+    g.scalar.dma_start(T.key64[16:32, :], T.key[:, :]).then_inc(S.keys, 16)
+    g.sync.dma_start(T.key64[32:48, :], T.key[:, :]).then_inc(S.keys, 16)
+    g.scalar.dma_start(T.key64[48:64, :], T.key[:, :]).then_inc(S.keys, 16)
+    g.sync.dma_start(T.xs[:, :], T.x[:, :]).then_inc(S.xin, 16)
+
+    g.iota(T.loi[:, :], [[0, 1]], 0, 256).then_inc(S.i_lo, 1)
+    g.iota(T.z[:, 0:128], [[-16, 2], [-16, 4], [0, 16]], 0, 1).then_inc(S.i_z, 1)
+    g.iota(T.z[:, 128:192], [[-1, 64]], 0, 1).then_inc(S.i_z, 1)
+    g.iota(T.zr[:, :], [[0, 8], [-1, 16]], 0, 1).then_inc(S.i_zr, 1)
+
+    V.memset(T.send[:, :], 0.0).then_inc(S.m_send, 1)
+    V.memset(T.zero16[:, :], 0.0).then_inc(S.m_small, 1)
+    V.memset(T.gp[:, 0:1], 0.0).then_inc(S.m_small, 1)
+    V.wait_ge(S.i_lo, 1)
+    V.tensor_scalar(T.lom[:, :], T.loi[:, :], 0xF000, None, A.bitwise_and).then_inc(S.c_lom, 1)
+    V.wait_ge(S.c_lom, 1)
+    V.tensor_copy(T.lo[:, :], T.lom[:, :]).then_inc(S.c_lo, 1)
+    V.wait_ge(S.c_lo, 1)
+    V.tensor_scalar(T.init[:, :], T.lo[:, :], float(CAP) / KR, -192.0, A.mult, A.add).then_inc(S.c_init, 1)
+    V.wait_ge(S.i_z, 2)
+    V.tensor_scalar(T.zs[:, :], T.z[:, :], 4, None, A.arith_shift_right).then_inc(S.c_zs, 1)
+    V.wait_ge(S.c_zs, 1)
+    V.tensor_scalar(T.e[:, :], T.zs[:, :], 0.0, None, A.is_equal).then_inc(S.c_e, 1)
+    V.wait_ge(S.c_e, 1)
+    V.tensor_tensor(T.l1[:, :], T.e[:, 0:64], T.e[:, 128:192], A.subtract).then_inc(S.c_l, 1)
+    V.tensor_tensor(T.l2[:, :], T.e[:, 128:192], T.e[:, 64:128], A.subtract).then_inc(S.c_l, 1)
+    V.wait_ge(S.i_zr, 1)
+    V.tensor_scalar(T.zra[:, :], T.zr[:, :], 15, None, A.bitwise_and).then_inc(S.c_zra, 1)
+    V.wait_ge(S.c_zra, 1)
+    V.tensor_scalar(T.rep[:, :], T.zra[:, :], 0.0, None, A.is_equal).then_inc(S.c_rep, 1)
+
+    V.wait_ge(S.keys, 64)
+    V.tensor_scalar(T.gp[:, 1:17], T.key64[:, :], T.lo[:, 0:1], None, A.is_ge).then_inc(S.v_g, 1)
+    V.tensor_scalar(T.g2[:, :], T.key64[:, :], T.lo[:, 0:1], float(KR), A.subtract, A.is_ge).then_inc(S.v_g2, 1)
+    PE.wait_ge(S.c_l, 2)
+    PE.wait_ge(S.m_small, 2)
+    PE.wait_ge(S.v_g, 1)
+    PE.matmul(T.pd[0:64, 0:16], T.l1[:, :], T.gp[:, 1:17], True, False)
+    PE.matmul(T.pd[0:64, 0:16], T.l2[:, :], T.gp[:, 0:16], False, True).then_inc(S.t_d, 1)
+    V.wait_ge(S.v_g, 1)
+    V.wait_ge(S.v_g2, 1)
+    V.tensor_tensor(T.oh[:, :], T.gp[:, 1:17], T.g2[:, :], A.subtract).then_inc(S.v_oh, 1)
+    V.wait_ge(S.m_small, 2)
+    V.wait_ge(S.c_init, 1)
+    V.wait_ge(S.t_d, 1)
+    V.tensor_tensor_scan(T.q[:, :], T.pd[0:64, 0:16], T.zero16[:, :], T.init[:, 0:1], A.add, A.add).then_inc(S.v_q, 1)
+    V.wait_ge(S.v_q, 1)
+    V.wait_ge(S.v_oh, 1)
+    V.tensor_tensor(T.prod[:, :], T.q[:, :], T.oh[:, :], A.mult).then_inc(S.v_prod, 1)
+    PE.wait_ge(S.c_rep, 1)
+    PE.wait_ge(S.v_prod, 1)
+    PE.matmul(T.ps[:, 0:16], T.rep[:, :], T.prod[:, :], True, True).then_inc(S.t_s, 1)
+    V.wait_ge(S.t_s, 1)
+    V.tensor_scalar(T.off[:, :], T.ps[:, 0:16], 192.0, None, A.add).then_inc(S.v_off, 1)
+
+    V.wait_ge(S.v_off, 1)
+    V.wait_ge(S.m_send, 1)
+    V.wait_ge(S.xin, 16)
+    V.tensor_copy(T.send[:, 0:N * CAP].indirect(T.off[:, 0:16]), T.xs[:, 0:TCOL]).then_inc(S.v_scat, 1)
+
+    plan = _plan(topo, cores, core)
+    transfers, total = [], 0
+    for dst, engines in plan.items():
+        d = T.rank_of(dst)
+        rid, pid = topo.addr(dst, core)
+        transfers.append(RemoteDMATransfer(
+            dst_ids=[DstId(rid=rid, pnc=pid)], dma_engine_mask=sum(1 << e for e in engines),
+            remote_sem=S.a_near if _same_chip(topo, core, dst) else S.a_far,
+            src=T.send[:, CAP * d:CAP * (d + 1)], dst=T.land[:, CAP * rank:CAP * (rank + 1)]))
+        total += len(engines)
+    g.wait_ge(S.v_scat, 1)
+    g.remote_dma_fused(transfers, local_sem=S.left)
+    V.wait_ge(S.v_scat, 1)
+    V.tensor_copy(T.land[:, CAP * rank:CAP * (rank + 1)], T.send[:, CAP * rank:CAP * (rank + 1)]).then_inc(S.v_own, 1)
+
+    near = [r for r in range(N) if _same_chip(topo, core, cores[r])]
+    far = [r for r in range(N) if r not in near]
+    for q, ranks, arr, st in ((g.scalar, near, S.a_near, S.st_near), (g.sync, far, S.a_far, S.st_far)):
+        expect = sum(len(_plan(topo, cores, cores[r])[core]) for r in ranks if r != rank)
+        if rank in ranks:
+            q.wait_ge(S.v_own, 1)
+        if expect:
+            q.wait_ge(arr, expect)
+        runs = _runs(ranks)
+        for a, b in runs:
+            q.dma_start(T.y[:, CAP * a:CAP * b], T.land[:, CAP * a:CAP * b]).then_inc(st, 16)
+        q.wait_ge(st, 16 * len(runs))
+    g.wait_ge(S.left, total)

@@ -1,27 +1,27 @@
 from concourse.bass import DstId, RemoteDMATransfer
-from concourse.mybir import AluOpType
+from concourse.mybir import AluOpType, ActivationFunctionType
 
 N, CAP, TCOL, KR = 4, 96, 256, 4096
-NEAR_SHARE = 8
+W = N * CAP
+ZW = 128
 
 SCRATCH = {
     "xs": ("sbuf", [128, TCOL], "float32"),
-    "send": ("sbuf", [128, N * CAP], "float32"),
-    "land": ("sbuf", [128, N * CAP], "float32"),
+    "send": ("sbuf", [128, W], "float32"),
+    "land": ("sbuf", [128, W], "float32"),
+    "zt": ("sbuf", [128, ZW], "bfloat16"),
     "key64": ("sbuf", [64, 16], "int32"),
-    "loi": ("sbuf", [64, 1], "int32"),
-    "lom": ("sbuf", [64, 1], "int32"),
     "lo": ("sbuf", [64, 1], "float32"),
     "init": ("sbuf", [64, 1], "float32"),
-    "z": ("sbuf", [64, 192], "int32"),
-    "zs": ("sbuf", [64, 192], "int32"),
-    "e": ("sbuf", [64, 192], "bfloat16"),
-    "l1": ("sbuf", [64, 64], "bfloat16"),
-    "l2": ("sbuf", [64, 64], "bfloat16"),
-    "zr": ("sbuf", [64, 128], "int32"),
+    "z": ("sbuf", [64, 208], "int32"),
+    "zs": ("sbuf", [64, 144], "int32"),
+    "e0": ("sbuf", [64, 64], "bfloat16"),
+    "e1n": ("sbuf", [64, 64], "bfloat16"),
+    "e2": ("sbuf", [64, 64], "bfloat16"),
     "zra": ("sbuf", [64, 128], "int32"),
     "rep": ("sbuf", [64, 128], "bfloat16"),
     "gp": ("sbuf", [64, 17], "bfloat16"),
+    "gd": ("sbuf", [64, 16], "bfloat16"),
     "g2": ("sbuf", [64, 16], "bfloat16"),
     "oh": ("sbuf", [64, 16], "bfloat16"),
     "zero16": ("sbuf", [64, 16], "float32"),
@@ -31,9 +31,14 @@ SCRATCH = {
     "pd": ("psum", [128, 512], "float32"),
     "ps": ("psum", [128, 512], "float32"),
 }
-SEMAPHORES = ["keys", "xin", "i_lo", "i_z", "i_zr", "m_send", "m_small", "c_lom", "c_lo", "c_init", "c_zs", "c_e", "c_l",
-              "c_zra", "c_rep", "v_g", "v_g2", "v_oh", "t_d", "v_q", "v_prod", "t_s", "v_off", "v_scat", "v_own",
-              "left", "a_near", "a_far", "st_near", "st_far"]
+SEMAPHORES = ["keys", "xin", "i_u", "i_v", "m_zt", "f_small", "f_send", "f_nb", "c_zsu", "c_zsv", "c_lo", "c_init", "c_e",
+              "c_zra", "c_rep", "v_g", "v_gd", "v_g2", "v_oh", "t_d", "v_q", "v_prod", "t_s", "v_off", "v_scat", "v_scn",
+              "left", "a_far", "st_own", "st_near", "st_far"]
+for _r in range(N):
+    SCRATCH["xn%d" % _r] = ("sbuf", [128, TCOL], "float32")
+    SCRATCH["on%d" % _r] = ("sbuf", [128, 16], "uint16")
+    SCRATCH["nb%d" % _r] = ("sbuf", [128, W], "float32")
+    SEMAPHORES += ["ax%d" % _r, "ao%d" % _r]
 
 
 def _bits(mask):
@@ -51,21 +56,31 @@ def _same_chip(topo, a, b):
     return topo.host(a) == topo.host(b) and topo.chip(a) == topo.chip(b)
 
 
-def _plan(topo, cores, src):
-    far = [c for c in cores if c != src and not _same_chip(topo, src, c)]
+def _groups(topo, cores, src):
     near = [c for c in cores if c != src and _same_chip(topo, src, c)]
-    used, plan = [], {}
-    for group, cap in ((far, None), (near, NEAR_SHARE)):
-        left = len(group)
-        for dst in group:
-            free = [e for e in _bits(topo.mask(src, dst)) if e not in used]
-            n = _pow2(len(free) // left)
-            if cap is not None:
-                n = min(n, cap)
-            plan[dst] = free[:n]
-            used += free[:n]
-            left -= 1
+    far = [c for c in cores if c != src and not _same_chip(topo, src, c)]
+    return near, far
+
+
+def _share(topo, src, group, avoid):
+    used, plan, left = list(avoid), {}, len(group)
+    for dst in group:
+        free = [e for e in _bits(topo.mask(src, dst)) if e not in used]
+        n = _pow2(len(free) // left)
+        plan[dst] = free[:n]
+        used += free[:n]
+        left -= 1
     return plan
+
+
+def _plans(topo, cores, src):
+    near, far = _groups(topo, cores, src)
+    p_far = _share(topo, src, far, [])
+    p_raw = _share(topo, src, near, [])
+    out = sorted(set(e for c in far for e in _bits(topo.mask(src, c))))
+    stay = [e for c in near for e in _bits(topo.mask(src, c)) if e not in out]
+    p_tab = _share(topo, src, near, out if len(stay) >= len(near) else [])
+    return p_raw, p_tab, p_far
 
 
 def _runs(ranks):
@@ -78,12 +93,30 @@ def _runs(ranks):
     return out
 
 
+def _call(g, topo, core, plan, items, local_sem):
+    transfers, total = [], 0
+    for dst, sem, src_ap, dst_ap in items:
+        rid, pid = topo.addr(dst, core)
+        transfers.append(RemoteDMATransfer(dst_ids=[DstId(rid=rid, pnc=pid)],
+                                           dma_engine_mask=sum(1 << e for e in plan[dst]),
+                                           remote_sem=sem, src=src_ap, dst=dst_ap))
+        total += len(plan[dst])
+    if transfers:
+        g.remote_dma_fused(transfers, local_sem=local_sem)
+    return total
+
+
 def rank_program(g, core, T, topo):
     rank = T.rank_of(core)
     if rank is None:
         return
-    S, V, PE, A = T.sem, g.vector, g.tensor, AluOpType
+    S, V, PE, ACT, A = T.sem, g.vector, g.tensor, g.scalar, AluOpType
+    COPY = ActivationFunctionType.Copy
     cores = list(T.cores)
+    near_c, far_c = _groups(topo, cores, core)
+    near = [T.rank_of(c) for c in near_c]
+    far = [T.rank_of(c) for c in far_c]
+    p_raw, p_tab, p_far = _plans(topo, cores, core)
 
     g.sync.dma_start(T.key64[0:16, :], T.key[:, :]).then_inc(S.keys, 16)
     g.scalar.dma_start(T.key64[16:32, :], T.key[:, :]).then_inc(S.keys, 16)
@@ -91,44 +124,61 @@ def rank_program(g, core, T, topo):
     g.scalar.dma_start(T.key64[48:64, :], T.key[:, :]).then_inc(S.keys, 16)
     g.sync.dma_start(T.xs[:, :], T.x[:, :]).then_inc(S.xin, 16)
 
-    g.iota(T.loi[:, :], [[0, 1]], 0, 256).then_inc(S.i_lo, 1)
-    g.iota(T.z[:, 0:128], [[-16, 2], [-16, 4], [0, 16]], 0, 1).then_inc(S.i_z, 1)
-    g.iota(T.z[:, 128:192], [[-1, 64]], 0, 1).then_inc(S.i_z, 1)
-    g.iota(T.zr[:, :], [[0, 8], [-1, 16]], 0, 1).then_inc(S.i_zr, 1)
+    g.iota(T.z[:, 0:80], [[-16, 5], [0, 16]], 0, 1).then_inc(S.i_u, 1)
+    g.iota(T.z[:, 80:208], [[-1, 128]], 0, 1).then_inc(S.i_v, 1)
 
-    V.memset(T.send[:, :], 0.0).then_inc(S.m_send, 1)
-    V.memset(T.zero16[:, :], 0.0).then_inc(S.m_small, 1)
-    V.memset(T.gp[:, 0:1], 0.0).then_inc(S.m_small, 1)
-    V.wait_ge(S.i_lo, 1)
-    V.tensor_scalar(T.lom[:, :], T.loi[:, :], 0xF000, None, A.bitwise_and).then_inc(S.c_lom, 1)
-    V.wait_ge(S.c_lom, 1)
-    V.tensor_copy(T.lo[:, :], T.lom[:, :]).then_inc(S.c_lo, 1)
-    V.wait_ge(S.c_lo, 1)
-    V.tensor_scalar(T.init[:, :], T.lo[:, :], float(CAP) / KR, -192.0, A.mult, A.add).then_inc(S.c_init, 1)
-    V.wait_ge(S.i_z, 2)
-    V.tensor_scalar(T.zs[:, :], T.z[:, :], 4, None, A.arith_shift_right).then_inc(S.c_zs, 1)
-    V.wait_ge(S.c_zs, 1)
-    V.tensor_scalar(T.e[:, :], T.zs[:, :], 0.0, None, A.is_equal).then_inc(S.c_e, 1)
-    V.wait_ge(S.c_e, 1)
-    V.tensor_tensor(T.l1[:, :], T.e[:, 0:64], T.e[:, 128:192], A.subtract).then_inc(S.c_l, 1)
-    V.tensor_tensor(T.l2[:, :], T.e[:, 128:192], T.e[:, 64:128], A.subtract).then_inc(S.c_l, 1)
-    V.wait_ge(S.i_zr, 1)
-    V.tensor_scalar(T.zra[:, :], T.zr[:, :], 15, None, A.bitwise_and).then_inc(S.c_zra, 1)
+    V.memset(T.zt[:, :], 0.0).then_inc(S.m_zt, 1)
+    ACT.wait_ge(S.m_zt, 1)
+    ACT.activation(T.gp[:, 0:1], T.zt[0:64, 0:1], COPY).then_inc(S.f_small, 1)
+    ACT.activation(T.zero16[:, :], T.zt[0:64, 0:16], COPY).then_inc(S.f_small, 1)
+    n_send = 0
+    for a in range(0, W, ZW):
+        b = min(a + ZW, W)
+        ACT.activation(T.send[:, a:b], T.zt[:, 0:b - a], COPY).then_inc(S.f_send, 1)
+        n_send += 1
+    n_nb = 0
+    for r in near:
+        for a in range(0, W, ZW):
+            b = min(a + ZW, W)
+            ACT.activation(T["nb%d" % r][:, a:b], T.zt[:, 0:b - a], COPY).then_inc(S.f_nb, 1)
+            n_nb += 1
+
+    V.wait_ge(S.i_u, 1)
+    V.tensor_scalar(T.zs[:, 0:80], T.z[:, 0:80], 4, None, A.arith_shift_right).then_inc(S.c_zsu, 1)
+    V.wait_ge(S.c_zsu, 1)
+    V.tensor_scalar(T.lo[:, :], T.zs[:, 0:1], float(KR), None, A.mult).then_inc(S.c_lo, 1)
+    V.tensor_scalar(T.init[:, :], T.zs[:, 0:1], float(CAP), -192.0, A.mult, A.add).then_inc(S.c_init, 1)
+    V.tensor_scalar(T.e0[:, :], T.zs[:, 0:64], 0.0, None, A.is_equal).then_inc(S.c_e, 1)
+    V.tensor_scalar(T.e1n[:, :], T.zs[:, 16:80], 0.0, -1.0, A.is_equal, A.mult).then_inc(S.c_e, 1)
+    V.wait_ge(S.i_v, 1)
+    V.tensor_scalar(T.zs[:, 80:144], T.z[:, 80:144], 4, None, A.arith_shift_right).then_inc(S.c_zsv, 1)
+    V.tensor_scalar(T.zra[:, :], T.z[:, 80:208], 15, None, A.bitwise_and).then_inc(S.c_zra, 1)
+    V.wait_ge(S.c_zsv, 1)
+    V.tensor_scalar(T.e2[:, :], T.zs[:, 80:144], 0.0, None, A.is_equal).then_inc(S.c_e, 1)
     V.wait_ge(S.c_zra, 1)
     V.tensor_scalar(T.rep[:, :], T.zra[:, :], 0.0, None, A.is_equal).then_inc(S.c_rep, 1)
 
+    total = 0
+    g.wait_ge(S.xin, 16)
+    total += _call(g, topo, core, p_raw,
+                   [(c, S["ax%d" % rank], T.xs[:, :], T["xn%d" % rank][:, :]) for c in near_c], S.left)
+
+    V.wait_ge(S.c_lo, 1)
     V.wait_ge(S.keys, 64)
     V.tensor_scalar(T.gp[:, 1:17], T.key64[:, :], T.lo[:, 0:1], None, A.is_ge).then_inc(S.v_g, 1)
-    V.tensor_scalar(T.g2[:, :], T.key64[:, :], T.lo[:, 0:1], float(KR), A.subtract, A.is_ge).then_inc(S.v_g2, 1)
-    PE.wait_ge(S.c_l, 2)
-    PE.wait_ge(S.m_small, 2)
+    PE.wait_ge(S.c_e, 3)
+    PE.wait_ge(S.f_small, 2)
     PE.wait_ge(S.v_g, 1)
-    PE.matmul(T.pd[0:64, 0:16], T.l1[:, :], T.gp[:, 1:17], True, False)
-    PE.matmul(T.pd[0:64, 0:16], T.l2[:, :], T.gp[:, 0:16], False, True).then_inc(S.t_d, 1)
+    PE.matmul(T.pd[0:64, 0:16], T.e0[:, :], T.gp[:, 1:17], True, False)
+    PE.matmul(T.pd[0:64, 0:16], T.e1n[:, :], T.gp[:, 0:16], False, False)
+    V.wait_ge(S.f_small, 2)
     V.wait_ge(S.v_g, 1)
+    V.tensor_tensor(T.gd[:, :], T.gp[:, 0:16], T.gp[:, 1:17], A.subtract).then_inc(S.v_gd, 1)
+    PE.wait_ge(S.v_gd, 1)
+    PE.matmul(T.pd[0:64, 0:16], T.e2[:, :], T.gd[:, :], False, True).then_inc(S.t_d, 1)
+    V.tensor_scalar(T.g2[:, :], T.key64[:, :], T.lo[:, 0:1], float(KR), A.subtract, A.is_ge).then_inc(S.v_g2, 1)
     V.wait_ge(S.v_g2, 1)
     V.tensor_tensor(T.oh[:, :], T.gp[:, 1:17], T.g2[:, :], A.subtract).then_inc(S.v_oh, 1)
-    V.wait_ge(S.m_small, 2)
     V.wait_ge(S.c_init, 1)
     V.wait_ge(S.t_d, 1)
     V.tensor_tensor_scan(T.q[:, :], T.pd[0:64, 0:16], T.zero16[:, :], T.init[:, 0:1], A.add, A.add).then_inc(S.v_q, 1)
@@ -141,36 +191,43 @@ def rank_program(g, core, T, topo):
     V.wait_ge(S.t_s, 1)
     V.tensor_scalar(T.off[:, :], T.ps[:, 0:16], 192.0, None, A.add).then_inc(S.v_off, 1)
 
+    g.wait_ge(S.v_off, 1)
+    total += _call(g, topo, core, p_tab,
+                   [(c, S["ao%d" % rank], T.off[:, :], T["on%d" % rank][:, :]) for c in near_c], S.left)
+
     V.wait_ge(S.v_off, 1)
-    V.wait_ge(S.m_send, 1)
+    V.wait_ge(S.f_send, n_send)
     V.wait_ge(S.xin, 16)
-    V.tensor_copy(T.send[:, 0:N * CAP].indirect(T.off[:, 0:16]), T.xs[:, 0:TCOL]).then_inc(S.v_scat, 1)
+    V.tensor_copy(T.send[:, 0:W].indirect(T.off[:, 0:16]), T.xs[:, 0:TCOL]).then_inc(S.v_scat, 1)
 
-    plan = _plan(topo, cores, core)
-    transfers, total = [], 0
-    for dst, engines in plan.items():
-        d = T.rank_of(dst)
-        rid, pid = topo.addr(dst, core)
-        transfers.append(RemoteDMATransfer(
-            dst_ids=[DstId(rid=rid, pnc=pid)], dma_engine_mask=sum(1 << e for e in engines),
-            remote_sem=S.a_near if _same_chip(topo, core, dst) else S.a_far,
-            src=T.send[:, CAP * d:CAP * (d + 1)], dst=T.land[:, CAP * rank:CAP * (rank + 1)]))
-        total += len(engines)
     g.wait_ge(S.v_scat, 1)
-    g.remote_dma_fused(transfers, local_sem=S.left)
-    V.wait_ge(S.v_scat, 1)
-    V.tensor_copy(T.land[:, CAP * rank:CAP * (rank + 1)], T.send[:, CAP * rank:CAP * (rank + 1)]).then_inc(S.v_own, 1)
+    total += _call(g, topo, core, p_far,
+                   [(c, S.a_far, T.send[:, CAP * T.rank_of(c):CAP * (T.rank_of(c) + 1)],
+                     T.land[:, CAP * rank:CAP * (rank + 1)]) for c in far_c], S.left)
 
-    near = [r for r in range(N) if _same_chip(topo, core, cores[r])]
-    far = [r for r in range(N) if r not in near]
-    for q, ranks, arr, st in ((g.scalar, near, S.a_near, S.st_near), (g.sync, far, S.a_far, S.st_far)):
-        expect = sum(len(_plan(topo, cores, cores[r])[core]) for r in ranks if r != rank)
-        if rank in ranks:
-            q.wait_ge(S.v_own, 1)
-        if expect:
-            q.wait_ge(arr, expect)
-        runs = _runs(ranks)
-        for a, b in runs:
-            q.dma_start(T.y[:, CAP * a:CAP * b], T.land[:, CAP * a:CAP * b]).then_inc(st, 16)
-        q.wait_ge(st, 16 * len(runs))
+    if near:
+        V.wait_ge(S.f_nb, n_nb)
+    for r in near:
+        q_raw, q_tab, _ = _plans(topo, cores, cores[r])
+        V.wait_ge(S["ax%d" % r], len(q_raw[core]))
+        V.wait_ge(S["ao%d" % r], len(q_tab[core]))
+        V.tensor_copy(T["nb%d" % r][:, 0:W].indirect(T["on%d" % r][:, 0:16]), T["xn%d" % r][:, 0:TCOL]).then_inc(S.v_scn, 1)
+
+    ACT.wait_ge(S.v_scat, 1)
+    g.scalar.dma_start(T.y[:, CAP * rank:CAP * (rank + 1)], T.send[:, CAP * rank:CAP * (rank + 1)]).then_inc(S.st_own, 16)
+    if near:
+        ACT.wait_ge(S.v_scn, len(near))
+    for r in near:
+        g.scalar.dma_start(T.y[:, CAP * r:CAP * (r + 1)], T["nb%d" % r][:, CAP * rank:CAP * (rank + 1)]).then_inc(S.st_near, 16)
+    expect = sum(len(_plans(topo, cores, cores[r])[2][core]) for r in far)
+    if far:
+        g.sync.wait_ge(S.a_far, expect)
+    runs = _runs(far)
+    for a, b in runs:
+        g.sync.dma_start(T.y[:, CAP * a:CAP * b], T.land[:, CAP * a:CAP * b]).then_inc(S.st_far, 16)
+    if runs:
+        g.sync.wait_ge(S.st_far, 16 * len(runs))
+    ACT.wait_ge(S.st_own, 16)
+    if near:
+        ACT.wait_ge(S.st_near, 16 * len(near))
     g.wait_ge(S.left, total)

from concourse.bass import DstId, RemoteDMATransfer
from concourse.mybir import AluOpType, ActivationFunctionType

N, CAP, TCOL, KR = 4, 96, 256, 4096
W = N * CAP
ZW = 128

SCRATCH = {
    "xs": ("sbuf", [128, TCOL], "float32"),
    "send": ("sbuf", [128, W], "float32"),
    "land": ("sbuf", [128, W], "float32"),
    "zt": ("sbuf", [128, ZW], "bfloat16"),
    "key64": ("sbuf", [64, 16], "int32"),
    "lo": ("sbuf", [64, 1], "float32"),
    "init": ("sbuf", [64, 1], "float32"),
    "z": ("sbuf", [64, 208], "int32"),
    "zs": ("sbuf", [64, 144], "int32"),
    "e0": ("sbuf", [64, 64], "bfloat16"),
    "e1n": ("sbuf", [64, 64], "bfloat16"),
    "e2": ("sbuf", [64, 64], "bfloat16"),
    "zra": ("sbuf", [64, 128], "int32"),
    "rep": ("sbuf", [64, 128], "bfloat16"),
    "gp": ("sbuf", [64, 17], "bfloat16"),
    "gd": ("sbuf", [64, 16], "bfloat16"),
    "g2": ("sbuf", [64, 16], "bfloat16"),
    "oh": ("sbuf", [64, 16], "bfloat16"),
    "zero16": ("sbuf", [64, 16], "float32"),
    "q": ("sbuf", [64, 16], "bfloat16"),
    "prod": ("sbuf", [64, 16], "bfloat16"),
    "off": ("sbuf", [128, 16], "uint16"),
    "pd": ("psum", [128, 512], "float32"),
    "ps": ("psum", [128, 512], "float32"),
}
SEMAPHORES = ["keys", "xin", "i_u", "i_v", "m_zt", "f_small", "f_send", "f_nb", "c_zsu", "c_zsv", "c_lo", "c_init", "c_e",
              "c_zra", "c_rep", "v_g", "v_gd", "v_g2", "v_oh", "t_d", "v_q", "v_prod", "t_s", "v_off", "v_scat", "v_scn",
              "left", "a_far", "st_own", "st_near", "st_far"]
for _r in range(N):
    SCRATCH["xn%d" % _r] = ("sbuf", [128, TCOL], "float32")
    SCRATCH["on%d" % _r] = ("sbuf", [128, 16], "uint16")
    SCRATCH["nb%d" % _r] = ("sbuf", [128, W], "float32")
    SEMAPHORES += ["ax%d" % _r, "ao%d" % _r]


def _bits(mask):
    return [e for e in range(mask.bit_length()) if (mask >> e) & 1]


def _pow2(n):
    p = 1
    while p * 2 <= n:
        p *= 2
    return p


def _same_chip(topo, a, b):
    return topo.host(a) == topo.host(b) and topo.chip(a) == topo.chip(b)


def _groups(topo, cores, src):
    near = [c for c in cores if c != src and _same_chip(topo, src, c)]
    far = [c for c in cores if c != src and not _same_chip(topo, src, c)]
    return near, far


def _share(topo, src, group, avoid):
    used, plan, left = list(avoid), {}, len(group)
    for dst in group:
        free = [e for e in _bits(topo.mask(src, dst)) if e not in used]
        n = _pow2(len(free) // left)
        plan[dst] = free[:n]
        used += free[:n]
        left -= 1
    return plan


def _plans(topo, cores, src):
    near, far = _groups(topo, cores, src)
    p_far = _share(topo, src, far, [])
    p_raw = _share(topo, src, near, [])
    out = sorted(set(e for c in far for e in _bits(topo.mask(src, c))))
    stay = [e for c in near for e in _bits(topo.mask(src, c)) if e not in out]
    p_tab = _share(topo, src, near, out if len(stay) >= len(near) else [])
    return p_raw, p_tab, p_far


def _runs(ranks):
    out = []
    for r in sorted(ranks):
        if out and out[-1][1] == r:
            out[-1][1] = r + 1
        else:
            out.append([r, r + 1])
    return out


def _call(g, topo, core, plan, items, local_sem):
    transfers, total = [], 0
    for dst, sem, src_ap, dst_ap in items:
        rid, pid = topo.addr(dst, core)
        transfers.append(RemoteDMATransfer(dst_ids=[DstId(rid=rid, pnc=pid)],
                                           dma_engine_mask=sum(1 << e for e in plan[dst]),
                                           remote_sem=sem, src=src_ap, dst=dst_ap))
        total += len(plan[dst])
    if transfers:
        g.remote_dma_fused(transfers, local_sem=local_sem)
    return total


def rank_program(g, core, T, topo):
    rank = T.rank_of(core)
    if rank is None:
        return
    S, V, PE, ACT, A = T.sem, g.vector, g.tensor, g.scalar, AluOpType
    COPY = ActivationFunctionType.Copy
    cores = list(T.cores)
    near_c, far_c = _groups(topo, cores, core)
    near = [T.rank_of(c) for c in near_c]
    far = [T.rank_of(c) for c in far_c]
    p_raw, p_tab, p_far = _plans(topo, cores, core)

    g.sync.dma_start(T.key64[0:16, :], T.key[:, :]).then_inc(S.keys, 16)
    g.scalar.dma_start(T.key64[16:32, :], T.key[:, :]).then_inc(S.keys, 16)
    g.sync.dma_start(T.key64[32:48, :], T.key[:, :]).then_inc(S.keys, 16)
    g.scalar.dma_start(T.key64[48:64, :], T.key[:, :]).then_inc(S.keys, 16)
    g.sync.dma_start(T.xs[:, :], T.x[:, :]).then_inc(S.xin, 16)

    g.iota(T.z[:, 0:80], [[-16, 5], [0, 16]], 0, 1).then_inc(S.i_u, 1)
    g.iota(T.z[:, 80:208], [[-1, 128]], 0, 1).then_inc(S.i_v, 1)

    V.memset(T.zt[:, :], 0.0).then_inc(S.m_zt, 1)
    ACT.wait_ge(S.m_zt, 1)
    ACT.activation(T.gp[:, 0:1], T.zt[0:64, 0:1], COPY).then_inc(S.f_small, 1)
    ACT.activation(T.zero16[:, :], T.zt[0:64, 0:16], COPY).then_inc(S.f_small, 1)
    n_send = 0
    for a in range(0, W, ZW):
        b = min(a + ZW, W)
        ACT.activation(T.send[:, a:b], T.zt[:, 0:b - a], COPY).then_inc(S.f_send, 1)
        n_send += 1
    n_nb = 0
    for r in near:
        for a in range(0, W, ZW):
            b = min(a + ZW, W)
            ACT.activation(T["nb%d" % r][:, a:b], T.zt[:, 0:b - a], COPY).then_inc(S.f_nb, 1)
            n_nb += 1

    V.wait_ge(S.i_u, 1)
    V.tensor_scalar(T.zs[:, 0:80], T.z[:, 0:80], 4, None, A.arith_shift_right).then_inc(S.c_zsu, 1)
    V.wait_ge(S.c_zsu, 1)
    V.tensor_scalar(T.lo[:, :], T.zs[:, 0:1], float(KR), None, A.mult).then_inc(S.c_lo, 1)
    V.tensor_scalar(T.init[:, :], T.zs[:, 0:1], float(CAP), -192.0, A.mult, A.add).then_inc(S.c_init, 1)
    V.tensor_scalar(T.e0[:, :], T.zs[:, 0:64], 0.0, None, A.is_equal).then_inc(S.c_e, 1)
    V.tensor_scalar(T.e1n[:, :], T.zs[:, 16:80], 0.0, -1.0, A.is_equal, A.mult).then_inc(S.c_e, 1)
    V.wait_ge(S.i_v, 1)
    V.tensor_scalar(T.zs[:, 80:144], T.z[:, 80:144], 4, None, A.arith_shift_right).then_inc(S.c_zsv, 1)
    V.tensor_scalar(T.zra[:, :], T.z[:, 80:208], 15, None, A.bitwise_and).then_inc(S.c_zra, 1)
    V.wait_ge(S.c_zsv, 1)
    V.tensor_scalar(T.e2[:, :], T.zs[:, 80:144], 0.0, None, A.is_equal).then_inc(S.c_e, 1)
    V.wait_ge(S.c_zra, 1)
    V.tensor_scalar(T.rep[:, :], T.zra[:, :], 0.0, None, A.is_equal).then_inc(S.c_rep, 1)

    total = 0
    g.wait_ge(S.xin, 16)
    total += _call(g, topo, core, p_raw,
                   [(c, S["ax%d" % rank], T.xs[:, :], T["xn%d" % rank][:, :]) for c in near_c], S.left)

    V.wait_ge(S.c_lo, 1)
    V.wait_ge(S.keys, 64)
    V.tensor_scalar(T.gp[:, 1:17], T.key64[:, :], T.lo[:, 0:1], None, A.is_ge).then_inc(S.v_g, 1)
    PE.wait_ge(S.c_e, 3)
    PE.wait_ge(S.f_small, 2)
    PE.wait_ge(S.v_g, 1)
    PE.matmul(T.pd[0:64, 0:16], T.e0[:, :], T.gp[:, 1:17], True, False)
    PE.matmul(T.pd[0:64, 0:16], T.e1n[:, :], T.gp[:, 0:16], False, False)
    V.wait_ge(S.f_small, 2)
    V.wait_ge(S.v_g, 1)
    V.tensor_tensor(T.gd[:, :], T.gp[:, 0:16], T.gp[:, 1:17], A.subtract).then_inc(S.v_gd, 1)
    PE.wait_ge(S.v_gd, 1)
    PE.matmul(T.pd[0:64, 0:16], T.e2[:, :], T.gd[:, :], False, True).then_inc(S.t_d, 1)
    V.tensor_scalar(T.g2[:, :], T.key64[:, :], T.lo[:, 0:1], float(KR), A.subtract, A.is_ge).then_inc(S.v_g2, 1)
    V.wait_ge(S.v_g2, 1)
    V.tensor_tensor(T.oh[:, :], T.gp[:, 1:17], T.g2[:, :], A.subtract).then_inc(S.v_oh, 1)
    V.wait_ge(S.c_init, 1)
    V.wait_ge(S.t_d, 1)
    V.tensor_tensor_scan(T.q[:, :], T.pd[0:64, 0:16], T.zero16[:, :], T.init[:, 0:1], A.add, A.add).then_inc(S.v_q, 1)
    V.wait_ge(S.v_q, 1)
    V.wait_ge(S.v_oh, 1)
    V.tensor_tensor(T.prod[:, :], T.q[:, :], T.oh[:, :], A.mult).then_inc(S.v_prod, 1)
    PE.wait_ge(S.c_rep, 1)
    PE.wait_ge(S.v_prod, 1)
    PE.matmul(T.ps[:, 0:16], T.rep[:, :], T.prod[:, :], True, True).then_inc(S.t_s, 1)
    V.wait_ge(S.t_s, 1)
    V.tensor_scalar(T.off[:, :], T.ps[:, 0:16], 192.0, None, A.add).then_inc(S.v_off, 1)

    g.wait_ge(S.v_off, 1)
    total += _call(g, topo, core, p_tab,
                   [(c, S["ao%d" % rank], T.off[:, :], T["on%d" % rank][:, :]) for c in near_c], S.left)

    V.wait_ge(S.v_off, 1)
    V.wait_ge(S.f_send, n_send)
    V.wait_ge(S.xin, 16)
    V.tensor_copy(T.send[:, 0:W].indirect(T.off[:, 0:16]), T.xs[:, 0:TCOL]).then_inc(S.v_scat, 1)

    g.wait_ge(S.v_scat, 1)
    total += _call(g, topo, core, p_far,
                   [(c, S.a_far, T.send[:, CAP * T.rank_of(c):CAP * (T.rank_of(c) + 1)],
                     T.land[:, CAP * rank:CAP * (rank + 1)]) for c in far_c], S.left)

    if near:
        V.wait_ge(S.f_nb, n_nb)
    for r in near:
        q_raw, q_tab, _ = _plans(topo, cores, cores[r])
        V.wait_ge(S["ax%d" % r], len(q_raw[core]))
        V.wait_ge(S["ao%d" % r], len(q_tab[core]))
        V.tensor_copy(T["nb%d" % r][:, 0:W].indirect(T["on%d" % r][:, 0:16]), T["xn%d" % r][:, 0:TCOL]).then_inc(S.v_scn, 1)

    ACT.wait_ge(S.v_scat, 1)
    g.scalar.dma_start(T.y[:, CAP * rank:CAP * (rank + 1)], T.send[:, CAP * rank:CAP * (rank + 1)]).then_inc(S.st_own, 16)
    if near:
        ACT.wait_ge(S.v_scn, len(near))
    for r in near:
        g.scalar.dma_start(T.y[:, CAP * r:CAP * (r + 1)], T["nb%d" % r][:, CAP * rank:CAP * (rank + 1)]).then_inc(S.st_near, 16)
    expect = sum(len(_plans(topo, cores, cores[r])[2][core]) for r in far)
    if far:
        g.sync.wait_ge(S.a_far, expect)
    runs = _runs(far)
    for a, b in runs:
        g.sync.dma_start(T.y[:, CAP * a:CAP * b], T.land[:, CAP * a:CAP * b]).then_inc(S.st_far, 16)
    if runs:
        g.sync.wait_ge(S.st_far, 16 * len(runs))
    ACT.wait_ge(S.st_own, 16)
    if near:
        ACT.wait_ge(S.st_near, 16 * len(near))
    g.wait_ge(S.left, total)
